import numpy as np
import ml_dtypes


def mxq(x, axis, fmt="e4m3"):
    dtype, down = {"e4m3": (ml_dtypes.float8_e4m3fn, 7), "e5m2": (ml_dtypes.float8_e5m2, 14)}[fmt]
    v = np.moveaxis(np.asarray(x, np.float32).astype(ml_dtypes.bfloat16).astype(np.float64), axis, -1)
    blocks = v.reshape(v.shape[:-1] + (-1, 32))
    amax = np.abs(blocks).max(-1, keepdims=True)
    byte = np.maximum(np.where(amax > 0, np.frexp(amax)[1] - 1 + 127, 0) - down, 1)
    scale = np.exp2(byte - 127.0)
    codes = (blocks / scale).astype(np.float32).astype(dtype).astype(np.float64)
    return np.moveaxis((codes * scale).reshape(v.shape), -1, axis)


WIDE = False


def mx_kscale(k):
    if not WIDE:
        return np.ones(k)
    levels = np.array([10, -10, 5, -5, 0])
    if k % 512:
        return np.exp2(np.random.permutation(np.resize(levels, k // 32))).repeat(32)
    a = np.empty((k // 512, 16))
    for p in range(k // 512):
        a[p, :8] = np.random.permutation(np.resize(levels, 8))
        for g in range(8):
            far = levels[np.abs(levels - a[p, g]) >= 10]
            a[p, g + 8] = far[np.random.randint(len(far))]
    return np.exp2(a.ravel()).repeat(32)


def f64(x):
    return np.asarray(x).astype(np.float64)


def striped(idx):
    return np.tile(np.asarray(idx).reshape(-1, 16).T, (8, 1)).astype(np.uint16)


def unstriped(offs):
    return offs[:16].T.reshape(-1).astype(np.int64)


E2M1 = np.array([0.0, 0.5, 1.0, 1.5, 2.0, 3.0, 4.0, 6.0, -0.0, -0.5, -1.0, -1.5, -2.0, -3.0, -4.0, -6.0])


def pack_weight(w, fmt):
    k, n = w.shape
    w = f64(np.asarray(w, np.float32).astype(ml_dtypes.bfloat16)).reshape(k // 32, 32, n)
    amax = np.abs(w).max(1)
    if fmt == "e4m3":
        byte = np.frexp(amax)[1] - 1 + 127 - 7
    else:
        mant, ex = np.frexp(amax / 6.0)
        byte = np.where(mant > 0.5, ex, ex - 1) + 127
    byte = np.clip(np.where(amax > 0, byte, 1), 1, 254)
    scaled = (w * np.exp2(127.0 - byte)[:, None, :]).reshape(k, n).astype(np.float32)
    by_word = np.ascontiguousarray(scaled.reshape(k // 512, 128, 4, n).transpose(0, 1, 3, 2))
    if fmt == "e4m3":
        words = by_word.astype(ml_dtypes.float8_e4m3fn).view(np.uint8)
    else:
        c = by_word.astype(ml_dtypes.float4_e2m1fn).view(np.uint8) & 0xF
        words = (c[..., 0::2] | (c[..., 1::2] << 4)).reshape(k // 512, 128, 2 * n)
    return np.ascontiguousarray(words), np.ascontiguousarray(byte.astype(np.uint8).reshape(k // 512, 16, n))


def unpack_weight(words, scales, fmt):
    g, _, n = scales.shape
    words = np.ascontiguousarray(words).reshape(g, 128, n, -1)
    if fmt == "e4m3":
        vals = words.view(ml_dtypes.float8_e4m3fn).astype(np.float64)
    else:
        nib = np.empty((g, 128, n, 4), np.uint8)
        nib[..., 0::2] = words & 0xF
        nib[..., 1::2] = words >> 4
        vals = E2M1[nib]
    vals = vals * np.repeat(np.exp2(scales.astype(np.float64) - 127.0), 8, axis=1)[..., None]
    return vals.transpose(0, 1, 3, 2).reshape(g * 512, n)


def sgn(shape):
    return np.random.uniform(0.5, 2.0, shape) * np.where(np.random.standard_normal(shape) < 0, -1.0, 1.0)


K, T, J, R, C, O, N = 512, 1024, 256, 512, 512, 256, 256


def setup_inputs():
    n = np.random.standard_normal
    idx = np.random.permutation(T)[:J]
    idx2 = np.random.permutation(C)[:J]
    idx3 = np.random.permutation(C)[:C]
    idx4 = np.random.permutation(C)[:O]
    fk = mx_kscale(K)
    fr = mx_kscale(R)
    xtp = pack_weight(n((K, T)) / fk[:, None], "e4m3")
    wp = pack_weight(n((K, R)) * 1 / np.sqrt(K) * fk[:, None], "e2m1")
    wbp = pack_weight(n((R, N)) * 1 / np.sqrt(R) / fr[:, None], "e2m1")
    return {
        "xt_words": xtp[0],
        "xt_scales": xtp[1],
        "w_words": wp[0],
        "w_scales": wp[1],
        "sa": (sgn((R, 1))).astype(np.float32),
        "sg": (0.25 * sgn((R, 1))).astype(np.float32),
        "lo": (np.random.uniform(-0.4, 0.4, (R, 1)) + np.log(fr)[:, None]).astype(np.float32),
        "wb_words": wbp[0],
        "wb_scales": wbp[1],
        "offs": striped(idx),
        "offs2": striped(idx2),
        "offs3": striped(idx3),
        "offs4": striped(idx4),
    }


def reference(xt_words, xt_scales, w_words, w_scales, sa, sg, lo, wb_words, wb_scales, offs, offs2, offs3, offs4):
    idx = unstriped(offs)
    idx2 = unstriped(offs2)
    idx3 = unstriped(offs3)
    idx4 = unstriped(offs4)
    xtu = unpack_weight(xt_words, xt_scales, "e4m3")
    wu = unpack_weight(w_words, w_scales, "e2m1")
    wbu = unpack_weight(wb_words, wb_scales, "e2m1")
    xtidxg = xtu[:, idx]
    a = wu.T @ xtidxg
    pw = np.zeros((R, C))
    pw[:, idx2] = a
    pg = np.maximum(pw, pw[:, idx3] * f64(sa))
    hid = np.exp(pg[:, idx4] * f64(sg) + f64(lo))
    hidq = mxq(hid, 0, "e4m3")
    p = wbu.T @ hidq
    return p

@@ -1,0 +1,168 @@
+from contextlib import ExitStack
+
+import concourse.mybir as mybir
+
+K, T, J, R, C, O, N = 512, 1024, 256, 512, 512, 256, 256
+FLOPS = 2 * K * R * J + 2 * R * N * O
+
+F32 = mybir.dt.float32
+BF16 = mybir.dt.bfloat16
+I32 = mybir.dt.int32
+U32 = mybir.dt.uint32
+U16 = mybir.dt.uint16
+U8 = mybir.dt.uint8
+FP8X4 = mybir.dt.float8_e4m3fn_x4
+FP4X4 = mybir.dt.float4_e2m1fn_x4
+ACT = mybir.ActivationFunctionType
+ALU = mybir.AluOpType
+
+P = 128
+PACK = 4
+BOARD = 2 * C
+HALF = O // 2
+
+
+def stage_scale_rows(queue, pool, scales, name):
+    width = scales.shape[1] // 4
+    rows = scales.rearrange("(q r) c -> r q c", r=4).bitcast(I32)
+    stage = pool.tile([P, 2, width], I32, name=name)
+    queue.dma_start(stage[0:4], rows[:, 0:2, :])
+    queue.dma_start(stage[64:68], rows[:, 2:4, :])
+    return stage
+
+
+def spread_scale_rows(nc, plane, stage):
+    words = plane[:].bitcast(I32)
+    for q in range(4):
+        src = 64 * (q // 2)
+        nc.vector.tensor_copy(words[32 * q : 32 * q + 4, :], stage[src : src + 4, q % 2, :])
+
+
+def tile_list_ladderexp_kernel(tc, xt_words, xt_scales, w_words, w_scales, sa, sg, lo, wb_words, wb_scales,
+                                  offs, offs2, offs3, offs4, out):
+    nc = tc.nc
+    with ExitStack() as ctx:
+        sb = ctx.enter_context(tc.tile_pool(name="sb", bufs=1))
+        ps = ctx.enter_context(tc.psum_pool(name="ps", bufs=1))
+
+        idx = sb.tile([P, J // 16], U16, name="idx")
+        idx2 = sb.tile([P, J // 16], U16, name="idx2")
+        idx3 = sb.tile([P, C // 16], U16, name="idx3")
+        idx4 = sb.tile([P, O // 16], U16, name="idx4")
+        xt = sb.tile([P, T], I32, name="xt")
+        w_raw = sb.tile([P, R], U16, name="w_raw")
+        wb = sb.tile([P, 2 * N], U8, name="wb", align_bytes=64)
+        sa_t = sb.tile([P, PACK], F32, name="sa_t")
+        sg_t = sb.tile([P, PACK], F32, name="sg_t")
+        lo_t = sb.tile([P, PACK], F32, name="lo_t")
+        xs_plane = sb.tile([P, T], U8, name="xs_plane")
+        ws_plane = sb.tile([P, R], U8, name="ws_plane")
+        wbs_plane = sb.tile([P, N], U8, name="wbs_plane", align_bytes=64)
+        pw = [sb.tile([P, BOARD], F32, name="pw%d" % t) for t in range(PACK)]
+
+        xs_stage = stage_scale_rows(nc.sync, sb, xt_scales[0], "xs_stage")
+        ws_stage = stage_scale_rows(nc.scalar, sb, w_scales[0], "ws_stage")
+        nc.sync.dma_start(idx[:], offs)
+        nc.sync.dma_start(xt[:], xt_words[0].rearrange("p n t -> p (n t)").bitcast(I32))
+        nc.scalar.dma_start(w_raw[:].bitcast(I32), w_words[0].bitcast(I32))
+        nc.sync.dma_start(idx2[:], offs2)
+        nc.sync.dma_start(idx3[:], offs3)
+        nc.sync.dma_start(sa_t[:], sa.rearrange("(p t) o -> p (t o)", t=PACK))
+        nc.sync.dma_start(idx4[:], offs4)
+        nc.sync.dma_start(sg_t[:], sg.rearrange("(p t) o -> p (t o)", t=PACK))
+        nc.sync.dma_start(lo_t[:], lo.rearrange("(p t) o -> p (t o)", t=PACK))
+        nc.sync.dma_start(wb[:].bitcast(I32), wb_words[0].bitcast(I32))
+
+        nc.vector.memset(xs_plane[:].bitcast(I32), 0)
+        nc.vector.memset(ws_plane[:].bitcast(I32), 0)
+        nc.vector.memset(wbs_plane[:].bitcast(I32), 0)
+        for t in range(PACK):
+            eng = nc.vector if t < 2 else nc.gpsimd
+            eng.memset(pw[t][:, 0:C], 0.0)
+        for q in range(4):
+            nc.sync.dma_start(wbs_plane[:].bitcast(I32)[32 * q : 32 * q + 4, :],
+                              wb_scales[0].bitcast(I32)[4 * q : 4 * q + 4, :])
+
+        xg = sb.tile([P, J], U32, name="xg", align_bytes=64)
+        xg_s = sb.tile([P, J], U8, name="xg_s", align_bytes=64)
+        w_t = sb.tile([P, PACK, P], U16, name="w_t", align_bytes=64)
+        ws_t = sb.tile([P, PACK, P], U8, name="ws_t", align_bytes=64)
+        spread_scale_rows(nc, xs_plane, xs_stage)
+        nc.vector.tensor_copy(xg_s[:], xs_plane[:].indirect(idx[:]))
+        spread_scale_rows(nc, ws_plane, ws_stage)
+        nc.vector.tensor_copy(ws_t[:], ws_plane[:].rearrange("p (m t) -> p t m", t=PACK))
+        nc.scalar.copy(w_t[:], w_raw[:].rearrange("p (m t) -> p t m", t=PACK))
+        nc.vector.tensor_copy(xg[:], xt[:].bitcast(U32).indirect(idx[:]))
+
+        a_ps = [ps.tile([P, J], F32, name="a_ps%d" % t) for t in range(PACK)]
+        for t in range(PACK):
+            nc.tensor.matmul_mx(a_ps[t][:], lhsT=w_t[:, t, :].bitcast(FP4X4), lhsT_scale=ws_t[:, t, :],
+                                rhs=xg[:].bitcast(FP8X4), rhs_scale=xg_s[:], start=True, stop=True)
+
+        a_sb = [sb.tile([P, J], F32, name="a_sb%d" % t) for t in range(PACK)]
+        prod = [sb.tile([P, C], F32, name="prod%d" % t) for t in range(PACK)]
+        pg = [sb.tile([P, C], F32, name="pg%d" % t) for t in range(PACK)]
+        hid = sb.tile([P, PACK * O], BF16, name="hid", align_bytes=64)
+
+        def place_on_vector(t):
+            nc.vector.tensor_copy(a_sb[t][:], a_ps[t][:])
+            nc.vector.tensor_copy(pw[t][:].indirect(idx2[:]), a_sb[t][:])
+
+        def place_on_scalar(t):
+            nc.scalar.copy(a_sb[t][:], a_ps[t][:])
+            nc.scalar.activation(pw[t][:].indirect(idx2[:]), a_sb[t][:], ACT.Copy)
+
+        def fetch_scaled(t):
+            nc.scalar.activation(prod[t][:], pw[t][:].indirect(idx3[:]), ACT.Copy, scale=sa_t[:, t : t + 1])
+
+        def keep_larger(t):
+            nc.vector.tensor_tensor(pg[t][:], pw[t][:, 0:C], prod[t][:], ALU.max)
+
+        def fetch_exp(t, o0, o1):
+            nc.scalar.activation(hid[:, PACK * o0 + t : PACK * o1 : PACK], pg[t][:].indirect(idx4[:, o0 // 16 : o1 // 16]),
+                                 ACT.Exp, bias=lo_t[:, t : t + 1], scale=sg_t[:, t : t + 1])
+
+        place_on_scalar(0)
+        place_on_vector(1)
+        fetch_scaled(0)
+        place_on_vector(2)
+        fetch_scaled(1)
+        keep_larger(0)
+        keep_larger(1)
+        fetch_scaled(2)
+        place_on_vector(3)
+        fetch_exp(0, 0, O)
+        fetch_exp(1, 0, O)
+        keep_larger(2)
+        fetch_scaled(3)
+        fetch_exp(2, 0, O)
+        keep_larger(3)
+        fetch_exp(3, 0, HALF)
+        fetch_exp(3, HALF, O)
+
+        hq = sb.tile([P, O], U32, name="hq", align_bytes=64)
+        hq_s = sb.tile([P, O], U8, name="hq_s", align_bytes=64)
+        res = sb.tile([P, 2, 2, HALF], F32, name="res")
+        first_ps = ps.tile([P, 2, HALF], F32, name="first_ps")
+        last_ps = [ps.tile([P, HALF], F32, name="last_ps%d" % h) for h in range(2)]
+
+        def second_product(dst, h, cols):
+            nc.tensor.matmul_mx(dst, lhsT=wb[:, 2 * P * h : 2 * P * (h + 1)].bitcast(FP4X4),
+                                lhsT_scale=wbs_plane[:, P * h : P * (h + 1)],
+                                rhs=hq[:, cols].bitcast(FP8X4), rhs_scale=hq_s[:, cols], start=True, stop=True)
+
+        for half in range(2):
+            cols = slice(HALF * half, HALF * (half + 1))
+            nc.vector.quantize_mx(hq[:, cols].bitcast(FP8X4), hq_s[:, cols], hid[:, PACK * cols.start : PACK * cols.stop])
+        cols = slice(0, HALF)
+        for h in range(2):
+            second_product(first_ps[:, h, :], h, cols)
+        nc.vector.tensor_copy(res[:, 0], first_ps[:])
+        nc.sync.dma_start(out.rearrange("(h p) o -> p h o", p=P)[:, :, cols], res[:, 0])
+        cols = slice(HALF, O)
+        for h in range(2):
+            second_product(last_ps[h][:], h, cols)
+        nc.scalar.copy(res[:, 1, 0, :], last_ps[0][:])
+        nc.scalar.dma_start(out[0:P, cols], res[:, 1, 0, :])
+        nc.vector.tensor_copy(res[:, 1, 1, :], last_ps[1][:])
+        nc.sync.dma_start(out[P : 2 * P, cols], res[:, 1, 1, :])

@@ -22,20 +22,8 @@ BOARD = 2 * C
 HALF = O // 2
 
 
-def stage_scale_rows(queue, pool, scales, name):
-    width = scales.shape[1] // 4
-    rows = scales.rearrange("(q r) c -> r q c", r=4).bitcast(I32)
-    stage = pool.tile([P, 2, width], I32, name=name)
-    queue.dma_start(stage[0:4], rows[:, 0:2, :])
-    queue.dma_start(stage[64:68], rows[:, 2:4, :])
-    return stage
-
-
-def spread_scale_rows(nc, plane, stage):
-    words = plane[:].bitcast(I32)
-    for q in range(4):
-        src = 64 * (q // 2)
-        nc.vector.tensor_copy(words[32 * q : 32 * q + 4, :], stage[src : src + 4, q % 2, :])
+def load_scale_rows(queue, plane, scales, q):
+    queue.dma_start(plane[:].bitcast(I32)[32 * q : 32 * q + 4, :], scales.bitcast(I32)[4 * q : 4 * q + 4, :])
 
 
 def tile_list_ladderexp_kernel(tc, xt_words, xt_scales, w_words, w_scales, sa, sg, lo, wb_words, wb_scales,
@@ -60,9 +48,18 @@ def tile_list_ladderexp_kernel(tc, xt_words, xt_scales, w_words, w_scales, sa, s
         wbs_plane = sb.tile([P, N], U8, name="wbs_plane", align_bytes=64)
         pw = [sb.tile([P, BOARD], F32, name="pw%d" % t) for t in range(PACK)]
 
-        xs_stage = stage_scale_rows(nc.sync, sb, xt_scales[0], "xs_stage")
-        ws_stage = stage_scale_rows(nc.scalar, sb, w_scales[0], "ws_stage")
+        ws_stage = sb.tile([4, 4, R // 4], I32, name="ws_stage")
+
+        nc.gpsimd.memset(xs_plane[:].bitcast(I32), 0)
+        nc.vector.memset(ws_plane[:].bitcast(I32), 0)
+        nc.vector.memset(wbs_plane[:].bitcast(I32), 0)
+        for t in range(PACK):
+            nc.vector.memset(pw[t][:, 0:C], 0.0)
+
+        nc.scalar.dma_start(ws_stage[:], w_scales[0].rearrange("(q r) c -> r q c", r=4).bitcast(I32))
         nc.sync.dma_start(idx[:], offs)
+        for q in range(4):
+            load_scale_rows(nc.sync if q < 2 else nc.scalar, xs_plane, xt_scales[0], q)
         nc.sync.dma_start(xt[:], xt_words[0].rearrange("p n t -> p (n t)").bitcast(I32))
         nc.scalar.dma_start(w_raw[:].bitcast(I32), w_words[0].bitcast(I32))
         nc.sync.dma_start(idx2[:], offs2)
@@ -72,45 +69,48 @@ def tile_list_ladderexp_kernel(tc, xt_words, xt_scales, w_words, w_scales, sa, s
         nc.sync.dma_start(sg_t[:], sg.rearrange("(p t) o -> p (t o)", t=PACK))
         nc.sync.dma_start(lo_t[:], lo.rearrange("(p t) o -> p (t o)", t=PACK))
         nc.sync.dma_start(wb[:].bitcast(I32), wb_words[0].bitcast(I32))
-
-        nc.vector.memset(xs_plane[:].bitcast(I32), 0)
-        nc.vector.memset(ws_plane[:].bitcast(I32), 0)
-        nc.vector.memset(wbs_plane[:].bitcast(I32), 0)
-        for t in range(PACK):
-            eng = nc.vector if t < 2 else nc.gpsimd
-            eng.memset(pw[t][:, 0:C], 0.0)
         for q in range(4):
-            nc.sync.dma_start(wbs_plane[:].bitcast(I32)[32 * q : 32 * q + 4, :],
-                              wb_scales[0].bitcast(I32)[4 * q : 4 * q + 4, :])
+            load_scale_rows(nc.sync, wbs_plane, wb_scales[0], q)
 
         xg = sb.tile([P, J], U32, name="xg", align_bytes=64)
         xg_s = sb.tile([P, J], U8, name="xg_s", align_bytes=64)
         w_t = sb.tile([P, PACK, P], U16, name="w_t", align_bytes=64)
         ws_t = sb.tile([P, PACK, P], U8, name="ws_t", align_bytes=64)
-        spread_scale_rows(nc, xs_plane, xs_stage)
-        nc.vector.tensor_copy(xg_s[:], xs_plane[:].indirect(idx[:]))
-        spread_scale_rows(nc, ws_plane, ws_stage)
-        nc.vector.tensor_copy(ws_t[:], ws_plane[:].rearrange("p (m t) -> p t m", t=PACK))
-        nc.scalar.copy(w_t[:], w_raw[:].rearrange("p (m t) -> p t m", t=PACK))
-        nc.vector.tensor_copy(xg[:], xt[:].bitcast(U32).indirect(idx[:]))
+        ws_dealt = ws_plane[:].rearrange("p (m t) -> p t m", t=PACK)
+        w_dealt = w_raw[:].rearrange("p (m t) -> p t m", t=PACK)
+        a_first = [ps.tile([P, J // 2], F32, name="a_first%d" % u) for u in range(2)]
+        a_ps = [None] + [ps.tile([P, J], F32, name="a_ps%d" % t) for t in range(1, PACK)]
 
-        a_ps = [ps.tile([P, J], F32, name="a_ps%d" % t) for t in range(PACK)]
-        for t in range(PACK):
-            nc.tensor.matmul_mx(a_ps[t][:], lhsT=w_t[:, t, :].bitcast(FP4X4), lhsT_scale=ws_t[:, t, :],
-                                rhs=xg[:].bitcast(FP8X4), rhs_scale=xg_s[:], start=True, stop=True)
+        def gather_tokens(u):
+            cols = slice(u * J // 2, (u + 1) * J // 2)
+            part = idx[:, cols.start // 16 : cols.stop // 16]
+            nc.vector.tensor_copy(xg[:, cols], xt[:].bitcast(U32).indirect(part))
+
+        def first_product(dst, t, cols):
+            nc.tensor.matmul_mx(dst, lhsT=w_t[:, t, :].bitcast(FP4X4), lhsT_scale=ws_t[:, t, :],
+                                rhs=xg[:, cols].bitcast(FP8X4), rhs_scale=xg_s[:, cols], start=True, stop=True)
+
+        for q in range(4):
+            nc.vector.tensor_copy(ws_plane[:].bitcast(I32)[32 * q : 32 * q + 4, :], ws_stage[:, q, :])
+        nc.vector.tensor_copy(ws_t[:], ws_dealt)
+        nc.vector.tensor_copy(xg_s[:], xs_plane[:].indirect(idx[:]))
+        nc.scalar.copy(w_t[:, 0, :], w_dealt[:, 0, :])
+        nc.scalar.copy(w_t[:, 1:PACK, :], w_dealt[:, 1:PACK, :])
+        gather_tokens(0)
+        first_product(a_first[0][:], 0, slice(0, J // 2))
+        gather_tokens(1)
+        first_product(a_ps[1][:], 1, slice(0, J))
+        first_product(a_first[1][:], 0, slice(J // 2, J))
+        for t in range(2, PACK):
+            first_product(a_ps[t][:], t, slice(0, J))
 
         a_sb = [sb.tile([P, J], F32, name="a_sb%d" % t) for t in range(PACK)]
         prod = [sb.tile([P, C], F32, name="prod%d" % t) for t in range(PACK)]
         pg = [sb.tile([P, C], F32, name="pg%d" % t) for t in range(PACK)]
-        hid = sb.tile([P, PACK * O], BF16, name="hid", align_bytes=64)
+        hid = [sb.tile([P, PACK * HALF], BF16, name="hid%d" % u, align_bytes=64) for u in range(2)]
 
-        def place_on_vector(t):
-            nc.vector.tensor_copy(a_sb[t][:], a_ps[t][:])
+        def scatter_on_vector(t):
             nc.vector.tensor_copy(pw[t][:].indirect(idx2[:]), a_sb[t][:])
-
-        def place_on_scalar(t):
-            nc.scalar.copy(a_sb[t][:], a_ps[t][:])
-            nc.scalar.activation(pw[t][:].indirect(idx2[:]), a_sb[t][:], ACT.Copy)
 
         def fetch_scaled(t):
             nc.scalar.activation(prod[t][:], pw[t][:].indirect(idx3[:]), ACT.Copy, scale=sa_t[:, t : t + 1])
@@ -118,27 +118,31 @@ def tile_list_ladderexp_kernel(tc, xt_words, xt_scales, w_words, w_scales, sa, s
         def keep_larger(t):
             nc.vector.tensor_tensor(pg[t][:], pw[t][:, 0:C], prod[t][:], ALU.max)
 
-        def fetch_exp(t, o0, o1):
-            nc.scalar.activation(hid[:, PACK * o0 + t : PACK * o1 : PACK], pg[t][:].indirect(idx4[:, o0 // 16 : o1 // 16]),
-                                 ACT.Exp, bias=lo_t[:, t : t + 1], scale=sg_t[:, t : t + 1])
+        def fetch_exp(t):
+            for u in range(2):
+                part = idx4[:, u * HALF // 16 : (u + 1) * HALF // 16]
+                nc.scalar.activation(hid[u][:, t : PACK * HALF : PACK], pg[t][:].indirect(part),
+                                     ACT.Exp, bias=lo_t[:, t : t + 1], scale=sg_t[:, t : t + 1])
 
-        place_on_scalar(0)
-        place_on_vector(1)
-        fetch_scaled(0)
-        place_on_vector(2)
-        fetch_scaled(1)
-        keep_larger(0)
-        keep_larger(1)
-        fetch_scaled(2)
-        place_on_vector(3)
-        fetch_exp(0, 0, O)
-        fetch_exp(1, 0, O)
-        keep_larger(2)
-        fetch_scaled(3)
-        fetch_exp(2, 0, O)
-        keep_larger(3)
-        fetch_exp(3, 0, HALF)
-        fetch_exp(3, HALF, O)
+        def scatter_first_tile(u):
+            cols = slice(u * J // 2, (u + 1) * J // 2)
+            nc.scalar.activation(pw[0][:].indirect(idx2[:, cols.start // 16 : cols.stop // 16]), a_sb[0][:, cols], ACT.Copy)
+
+        nc.scalar.copy(a_sb[0][:, 0 : J // 2], a_first[0][:])
+        nc.vector.tensor_copy(a_sb[1][:], a_ps[1][:])
+        nc.vector.tensor_copy(a_sb[0][:, J // 2 : J], a_first[1][:])
+        scatter_first_tile(0)
+        nc.scalar.copy(a_sb[2][:], a_ps[2][:])
+        scatter_first_tile(1)
+        nc.scalar.copy(a_sb[3][:], a_ps[3][:])
+        for t in range(1, PACK):
+            scatter_on_vector(t)
+        for t in range(PACK):
+            fetch_scaled(t)
+        for t in range(PACK):
+            keep_larger(t)
+        for t in range(PACK):
+            fetch_exp(t)
 
         hq = sb.tile([P, O], U32, name="hq", align_bytes=64)
         hq_s = sb.tile([P, O], U8, name="hq_s", align_bytes=64)
@@ -153,7 +157,7 @@ def tile_list_ladderexp_kernel(tc, xt_words, xt_scales, w_words, w_scales, sa, s
 
         for half in range(2):
             cols = slice(HALF * half, HALF * (half + 1))
-            nc.vector.quantize_mx(hq[:, cols].bitcast(FP8X4), hq_s[:, cols], hid[:, PACK * cols.start : PACK * cols.stop])
+            nc.vector.quantize_mx(hq[:, cols].bitcast(FP8X4), hq_s[:, cols], hid[half][:])
         cols = slice(0, HALF)
         for h in range(2):
             second_product(first_ps[:, h, :], h, cols)

from contextlib import ExitStack

import concourse.mybir as mybir

K, T, J, R, C, O, N = 512, 1024, 256, 512, 512, 256, 256
FLOPS = 2 * K * R * J + 2 * R * N * O

F32 = mybir.dt.float32
BF16 = mybir.dt.bfloat16
I32 = mybir.dt.int32
U32 = mybir.dt.uint32
U16 = mybir.dt.uint16
U8 = mybir.dt.uint8
FP8X4 = mybir.dt.float8_e4m3fn_x4
FP4X4 = mybir.dt.float4_e2m1fn_x4
ACT = mybir.ActivationFunctionType
ALU = mybir.AluOpType

P = 128
PACK = 4
BOARD = 2 * C
HALF = O // 2


def load_scale_rows(queue, plane, scales, q):
    queue.dma_start(plane[:].bitcast(I32)[32 * q : 32 * q + 4, :], scales.bitcast(I32)[4 * q : 4 * q + 4, :])


def tile_list_ladderexp_kernel(tc, xt_words, xt_scales, w_words, w_scales, sa, sg, lo, wb_words, wb_scales,
                                  offs, offs2, offs3, offs4, out):
    nc = tc.nc
    with ExitStack() as ctx:
        sb = ctx.enter_context(tc.tile_pool(name="sb", bufs=1))
        ps = ctx.enter_context(tc.psum_pool(name="ps", bufs=1))

        idx = sb.tile([P, J // 16], U16, name="idx")
        idx2 = sb.tile([P, J // 16], U16, name="idx2")
        idx3 = sb.tile([P, C // 16], U16, name="idx3")
        idx4 = sb.tile([P, O // 16], U16, name="idx4")
        xt = sb.tile([P, T], I32, name="xt")
        w_raw = sb.tile([P, R], U16, name="w_raw")
        wb = sb.tile([P, 2 * N], U8, name="wb", align_bytes=64)
        sa_t = sb.tile([P, PACK], F32, name="sa_t")
        sg_t = sb.tile([P, PACK], F32, name="sg_t")
        lo_t = sb.tile([P, PACK], F32, name="lo_t")
        xs_plane = sb.tile([P, T], U8, name="xs_plane")
        ws_plane = sb.tile([P, R], U8, name="ws_plane")
        wbs_plane = sb.tile([P, N], U8, name="wbs_plane", align_bytes=64)
        pw = [sb.tile([P, BOARD], F32, name="pw%d" % t) for t in range(PACK)]

        ws_stage = sb.tile([4, 4, R // 4], I32, name="ws_stage")

        nc.gpsimd.memset(xs_plane[:].bitcast(I32), 0)
        nc.vector.memset(ws_plane[:].bitcast(I32), 0)
        nc.vector.memset(wbs_plane[:].bitcast(I32), 0)
        for t in range(PACK):
            nc.vector.memset(pw[t][:, 0:C], 0.0)

        nc.scalar.dma_start(ws_stage[:], w_scales[0].rearrange("(q r) c -> r q c", r=4).bitcast(I32))
        nc.sync.dma_start(idx[:], offs)
        for q in range(4):
            load_scale_rows(nc.sync if q < 2 else nc.scalar, xs_plane, xt_scales[0], q)
        nc.sync.dma_start(xt[:], xt_words[0].rearrange("p n t -> p (n t)").bitcast(I32))
        nc.scalar.dma_start(w_raw[:].bitcast(I32), w_words[0].bitcast(I32))
        nc.sync.dma_start(idx2[:], offs2)
        nc.sync.dma_start(idx3[:], offs3)
        nc.sync.dma_start(sa_t[:], sa.rearrange("(p t) o -> p (t o)", t=PACK))
        nc.sync.dma_start(idx4[:], offs4)
        nc.sync.dma_start(sg_t[:], sg.rearrange("(p t) o -> p (t o)", t=PACK))
        nc.sync.dma_start(lo_t[:], lo.rearrange("(p t) o -> p (t o)", t=PACK))
        nc.sync.dma_start(wb[:].bitcast(I32), wb_words[0].bitcast(I32))
        for q in range(4):
            load_scale_rows(nc.sync, wbs_plane, wb_scales[0], q)

        xg = sb.tile([P, J], U32, name="xg", align_bytes=64)
        xg_s = sb.tile([P, J], U8, name="xg_s", align_bytes=64)
        w_t = sb.tile([P, PACK, P], U16, name="w_t", align_bytes=64)
        ws_t = sb.tile([P, PACK, P], U8, name="ws_t", align_bytes=64)
        ws_dealt = ws_plane[:].rearrange("p (m t) -> p t m", t=PACK)
        w_dealt = w_raw[:].rearrange("p (m t) -> p t m", t=PACK)
        a_first = [ps.tile([P, J // 2], F32, name="a_first%d" % u) for u in range(2)]
        a_ps = [None] + [ps.tile([P, J], F32, name="a_ps%d" % t) for t in range(1, PACK)]

        def gather_tokens(u):
            cols = slice(u * J // 2, (u + 1) * J // 2)
            part = idx[:, cols.start // 16 : cols.stop // 16]
            nc.vector.tensor_copy(xg[:, cols], xt[:].bitcast(U32).indirect(part))

        def first_product(dst, t, cols):
            nc.tensor.matmul_mx(dst, lhsT=w_t[:, t, :].bitcast(FP4X4), lhsT_scale=ws_t[:, t, :],
                                rhs=xg[:, cols].bitcast(FP8X4), rhs_scale=xg_s[:, cols], start=True, stop=True)

        for q in range(4):
            nc.vector.tensor_copy(ws_plane[:].bitcast(I32)[32 * q : 32 * q + 4, :], ws_stage[:, q, :])
        nc.vector.tensor_copy(ws_t[:], ws_dealt)
        nc.vector.tensor_copy(xg_s[:], xs_plane[:].indirect(idx[:]))
        nc.scalar.copy(w_t[:, 0, :], w_dealt[:, 0, :])
        nc.scalar.copy(w_t[:, 1:PACK, :], w_dealt[:, 1:PACK, :])
        gather_tokens(0)
        first_product(a_first[0][:], 0, slice(0, J // 2))
        gather_tokens(1)
        first_product(a_ps[1][:], 1, slice(0, J))
        first_product(a_first[1][:], 0, slice(J // 2, J))
        for t in range(2, PACK):
            first_product(a_ps[t][:], t, slice(0, J))

        a_sb = [sb.tile([P, J], F32, name="a_sb%d" % t) for t in range(PACK)]
        prod = [sb.tile([P, C], F32, name="prod%d" % t) for t in range(PACK)]
        pg = [sb.tile([P, C], F32, name="pg%d" % t) for t in range(PACK)]
        hid = [sb.tile([P, PACK * HALF], BF16, name="hid%d" % u, align_bytes=64) for u in range(2)]

        def scatter_on_vector(t):
            nc.vector.tensor_copy(pw[t][:].indirect(idx2[:]), a_sb[t][:])

        def fetch_scaled(t):
            nc.scalar.activation(prod[t][:], pw[t][:].indirect(idx3[:]), ACT.Copy, scale=sa_t[:, t : t + 1])

        def keep_larger(t):
            nc.vector.tensor_tensor(pg[t][:], pw[t][:, 0:C], prod[t][:], ALU.max)

        def fetch_exp(t):
            for u in range(2):
                part = idx4[:, u * HALF // 16 : (u + 1) * HALF // 16]
                nc.scalar.activation(hid[u][:, t : PACK * HALF : PACK], pg[t][:].indirect(part),
                                     ACT.Exp, bias=lo_t[:, t : t + 1], scale=sg_t[:, t : t + 1])

        def scatter_first_tile(u):
            cols = slice(u * J // 2, (u + 1) * J // 2)
            nc.scalar.activation(pw[0][:].indirect(idx2[:, cols.start // 16 : cols.stop // 16]), a_sb[0][:, cols], ACT.Copy)

        nc.scalar.copy(a_sb[0][:, 0 : J // 2], a_first[0][:])
        nc.vector.tensor_copy(a_sb[1][:], a_ps[1][:])
        nc.vector.tensor_copy(a_sb[0][:, J // 2 : J], a_first[1][:])
        scatter_first_tile(0)
        nc.scalar.copy(a_sb[2][:], a_ps[2][:])
        scatter_first_tile(1)
        nc.scalar.copy(a_sb[3][:], a_ps[3][:])
        for t in range(1, PACK):
            scatter_on_vector(t)
        for t in range(PACK):
            fetch_scaled(t)
        for t in range(PACK):
            keep_larger(t)
        for t in range(PACK):
            fetch_exp(t)

        hq = sb.tile([P, O], U32, name="hq", align_bytes=64)
        hq_s = sb.tile([P, O], U8, name="hq_s", align_bytes=64)
        res = sb.tile([P, 2, 2, HALF], F32, name="res")
        first_ps = ps.tile([P, 2, HALF], F32, name="first_ps")
        last_ps = [ps.tile([P, HALF], F32, name="last_ps%d" % h) for h in range(2)]

        def second_product(dst, h, cols):
            nc.tensor.matmul_mx(dst, lhsT=wb[:, 2 * P * h : 2 * P * (h + 1)].bitcast(FP4X4),
                                lhsT_scale=wbs_plane[:, P * h : P * (h + 1)],
                                rhs=hq[:, cols].bitcast(FP8X4), rhs_scale=hq_s[:, cols], start=True, stop=True)

        for half in range(2):
            cols = slice(HALF * half, HALF * (half + 1))
            nc.vector.quantize_mx(hq[:, cols].bitcast(FP8X4), hq_s[:, cols], hid[half][:])
        cols = slice(0, HALF)
        for h in range(2):
            second_product(first_ps[:, h, :], h, cols)
        nc.vector.tensor_copy(res[:, 0], first_ps[:])
        nc.sync.dma_start(out.rearrange("(h p) o -> p h o", p=P)[:, :, cols], res[:, 0])
        cols = slice(HALF, O)
        for h in range(2):
            second_product(last_ps[h][:], h, cols)
        nc.scalar.copy(res[:, 1, 0, :], last_ps[0][:])
        nc.scalar.dma_start(out[0:P, cols], res[:, 1, 0, :])
        nc.vector.tensor_copy(res[:, 1, 1, :], last_ps[1][:])
        nc.sync.dma_start(out[P : 2 * P, cols], res[:, 1, 1, :])
